import numpy as np
import ml_dtypes


def mxq(x, axis, fmt="e4m3"):
    dtype, down = {"e4m3": (ml_dtypes.float8_e4m3fn, 7), "e5m2": (ml_dtypes.float8_e5m2, 14)}[fmt]
    v = np.moveaxis(np.asarray(x, np.float32).astype(ml_dtypes.bfloat16).astype(np.float64), axis, -1)
    blocks = v.reshape(v.shape[:-1] + (-1, 32))
    amax = np.abs(blocks).max(-1, keepdims=True)
    byte = np.maximum(np.where(amax > 0, np.frexp(amax)[1] - 1 + 127, 0) - down, 1)
    scale = np.exp2(byte - 127.0)
    codes = (blocks / scale).astype(np.float32).astype(dtype).astype(np.float64)
    return np.moveaxis((codes * scale).reshape(v.shape), -1, axis)


WIDE = False


def mx_kscale(k):
    if not WIDE:
        return np.ones(k)
    levels = np.array([10, -10, 5, -5, 0])
    if k % 512:
        return np.exp2(np.random.permutation(np.resize(levels, k // 32))).repeat(32)
    a = np.empty((k // 512, 16))
    for p in range(k // 512):
        a[p, :8] = np.random.permutation(np.resize(levels, 8))
        for g in range(8):
            far = levels[np.abs(levels - a[p, g]) >= 10]
            a[p, g + 8] = far[np.random.randint(len(far))]
    return np.exp2(a.ravel()).repeat(32)


BF16 = ml_dtypes.bfloat16


def bf(x):
    return np.asarray(x, np.float32).astype(BF16)


def f64(x):
    return np.asarray(x).astype(np.float64)


E2M1 = np.array([0.0, 0.5, 1.0, 1.5, 2.0, 3.0, 4.0, 6.0, -0.0, -0.5, -1.0, -1.5, -2.0, -3.0, -4.0, -6.0])


def pack_weight(w, fmt):
    k, n = w.shape
    w = f64(bf(w)).reshape(k // 32, 32, n)
    amax = np.abs(w).max(1)
    if fmt == "e4m3":
        byte = np.frexp(amax)[1] - 1 + 127 - 7
    else:
        mant, ex = np.frexp(amax / 6.0)
        byte = np.where(mant > 0.5, ex, ex - 1) + 127
    byte = np.clip(np.where(amax > 0, byte, 1), 1, 254)
    scaled = (w * np.exp2(127.0 - byte)[:, None, :]).reshape(k, n).astype(np.float32)
    by_word = np.ascontiguousarray(scaled.reshape(k // 512, 128, 4, n).transpose(0, 1, 3, 2))
    if fmt == "e4m3":
        words = by_word.astype(ml_dtypes.float8_e4m3fn).view(np.uint8)
    else:
        c = by_word.astype(ml_dtypes.float4_e2m1fn).view(np.uint8) & 0xF
        words = c[..., 0::2] | (c[..., 1::2] << 4)
    return np.ascontiguousarray(words), np.ascontiguousarray(byte.astype(np.uint8).reshape(k // 512, 16, n))


def unpack_weight(words, scales, fmt):
    g, p, n, _ = words.shape
    if fmt == "e4m3":
        vals = np.ascontiguousarray(words).view(ml_dtypes.float8_e4m3fn).astype(np.float64)
    else:
        nib = np.empty((g, p, n, 4), np.uint8)
        nib[..., 0::2] = words & 0xF
        nib[..., 1::2] = words >> 4
        vals = E2M1[nib]
    vals = vals * np.repeat(np.exp2(scales.astype(np.float64) - 127.0), 8, axis=1)[..., None]
    return vals.transpose(0, 1, 3, 2).reshape(g * 512, n)

E4M3FN = np.array([(-1.0 if i & 128 else 1.0) * ((1.0 + (i & 7) / 8.0) * 2.0 ** (((i >> 3) & 15) - 7) if i & 120 else (i & 7) * 2.0 ** -9) for i in range(256)])


def e4m3fn_bytes(y):
    return np.clip(np.asarray(y, np.float64), -448.0, 448.0).astype(np.float32).astype(ml_dtypes.float8_e4m3fn).view(np.uint8)


def e4m3fn_values(b):
    return E4M3FN[b]


N, D, F = 512, 512, 1024


def erf(a):
    c = np.clip(a, -6.0, 6.0)
    term = c
    total = c
    for n in range(1, 150):
        term = term * (2.0 * c * c / (2 * n + 1))
        total = total + term
    r = 2.0 / np.sqrt(np.pi) * np.exp(-c * c) * total
    return np.where(np.abs(a) > 6.0, np.sign(a), r)


def gelu_and_slope(g):
    phi = 0.5 * (1.0 + erf(g / np.sqrt(2.0)))
    act = g * phi
    dact = phi + g * np.exp(-(g * g) / 2.0) / np.sqrt(2.0 * np.pi)
    return act, dact


def draw0():
    s, t = mx_kscale(D), mx_kscale(F)
    cd, cf = 1.0 / np.sqrt(D), 1.0 / np.sqrt(F)
    x = bf(np.random.standard_normal((N, D)) * s)
    wg_words, wg_scales = pack_weight(np.random.standard_normal((D, F)) * cd / s[:, None], "e4m3")
    vg = bf(np.random.standard_normal((D, F)) * cd / s[:, None])
    wu_words, wu_scales = pack_weight(np.random.standard_normal((D, F)) * cd / s[:, None] * t, "e4m3")
    vu = bf(np.random.standard_normal((D, F)) * cd / s[:, None] * t)
    wd_words, wd_scales = pack_weight(np.random.standard_normal((F, D)) * cf / t[:, None], "e4m3")
    vd = bf(np.random.standard_normal((F, D)) * cf / t[:, None])
    return {
        "x": x,
        "wg_words": wg_words,
        "wg_scales": wg_scales,
        "vg": vg,
        "wu_words": wu_words,
        "wu_scales": wu_scales,
        "vu": vu,
        "wd_words": wd_words,
        "wd_scales": wd_scales,
        "vd": vd,
    }


def core(x, wg_words, wg_scales, vg, wu_words, wu_scales, vu, wd_words, wd_scales, vd):
    xq = mxq(f64(x), 1, "e4m3")
    g = xq @ unpack_weight(wg_words, wg_scales, "e4m3")
    dg = xq @ mxq(f64(vg), 0, "e4m3")
    u = xq @ unpack_weight(wu_words, wu_scales, "e4m3")
    du = xq @ mxq(f64(vu), 0, "e4m3")
    act, dact = gelu_and_slope(g)
    h = act * u
    dh = dact * dg * u + act * du
    dy = (mxq(dh, 1, "e4m3") @ unpack_weight(wd_words, wd_scales, "e4m3")) + (mxq(h, 1, "e4m3") @ mxq(f64(vd), 0, "e4m3"))
    return dy


def setup_inputs():
    drawn = draw0()
    full = np.asarray(drawn['vg']).astype(np.float64)
    scale = (np.abs(full).reshape(512, 8, 128).max(axis=(2,)) / 448.0).astype(np.float32)
    given = {}
    for key, value in drawn.items():
        if key == 'vg':
            given['vg_bytes'] = e4m3fn_bytes(full / np.repeat(scale.astype(np.float64), 128, axis=1))
            given['vg_scale'] = scale
        else:
            given[key] = value
    return given


def reference(x, wg_words, wg_scales, vg_bytes, vg_scale, wu_words, wu_scales, vu, wd_words, wd_scales, vd):
    return core(x, wg_words, wg_scales, e4m3fn_values(vg_bytes) * np.repeat(vg_scale.astype(np.float64), 128, axis=1), wu_words, wu_scales, vu, wd_words, wd_scales, vd)

@@ -1,0 +1,308 @@
+from contextlib import ExitStack
+
+import concourse.mybir as mybir
+from concourse.masks import make_identity
+
+TOK, D, F = 512, 512, 1024
+FLOPS = 2 * TOK * D * F * 6
+
+F32 = mybir.dt.float32
+BF16 = mybir.dt.bfloat16
+I32 = mybir.dt.int32
+U32 = mybir.dt.uint32
+U8 = mybir.dt.uint8
+F8 = mybir.dt.float8_e4m3fn
+FP8X4 = mybir.dt.float8_e4m3fn_x4
+ACT = mybir.ActivationFunctionType
+ALU = mybir.AluOpType
+
+P = 128
+TT = TOK // P
+FG = F // 512
+CH = 512
+VW = 1
+NA = 3
+TAU = 2.5e-10
+LOG_C = -0.9189385332046727
+
+
+def tile_forwardgradientgegluweighttangent_d1p_kernel(
+    tc, x, wg_words, wg_scales, vg_bytes, vg_scale, wu_words, wu_scales, vu, wd_words, wd_scales, vd, out
+):
+    nc = tc.nc
+    with ExitStack() as ctx:
+        keep = ctx.enter_context(tc.tile_pool(name="keep", bufs=1))
+        work = ctx.enter_context(tc.tile_pool(name="work", bufs=2))
+        psum = ctx.enter_context(tc.psum_pool(name="psum", bufs=2))
+        ctx.enter_context(tc.manual_schedule())
+
+        def keep_tile(name, cols, dtype):
+            return keep.tile([P, cols], dtype, name=name, align_bytes=64)
+
+        x_raw = []
+        for h in range(2):
+            t = keep_tile(f"x_raw{h}", 2 * D, BF16)
+            nc.sync.dma_start(
+                out=t[:].rearrange("p (b d) -> p b d", b=2),
+                in_=x.rearrange("(h b p) d -> h p b d", b=2, p=P)[h],
+            )
+            x_raw.append(t)
+        vg_s = keep_tile("vg_s", 32, F32)
+        nc.sync.dma_start(out=vg_s[:], in_=vg_scale.rearrange("(p j) s -> p (j s)", j=4))
+        vg_b = keep_tile("vg_b", 4 * F, U8)
+        nc.sync.dma_start(out=vg_b[:], in_=vg_bytes.rearrange("(p j) f -> p (j f)", j=4))
+        wg_raw = keep_tile("wg_raw", F, I32)
+        nc.sync.dma_start(out=wg_raw[:], in_=wg_words[0].rearrange("p n t -> p (n t)").bitcast(I32))
+
+        warm = keep_tile("warm", 1, F32)
+        nc.vector.memset(warm[:], 0.0)
+        nc.scalar.activation(out=warm[:], in_=warm[:], func=ACT.Gelu)
+        gu_scales_raw = keep_tile("gu_scales_raw", F, U8)
+        wd_sc = keep_tile("wd_sc", FG * D, U8)
+        nc.vector.memset(gu_scales_raw[:].bitcast(I32), 0)
+        nc.vector.memset(wd_sc[:].bitcast(I32), 0)
+        ident = keep_tile("ident", P, F32)
+        make_identity(nc, ident[:])
+        for first, scales in ((0, wg_scales), (4, wu_scales)):
+            for quad in range(4):
+                rows = slice(32 * quad + first, 32 * quad + first + 4)
+                nc.scalar.dma_start(
+                    out=gu_scales_raw[rows, :].bitcast(I32),
+                    in_=scales[0, 4 * quad : 4 * quad + 4, :].bitcast(I32),
+                )
+
+        vu_raw = keep_tile("vu_raw", 4 * F, BF16)
+        nc.sync.dma_start(out=vu_raw[:], in_=vu.rearrange("(p j) f -> p (j f)", j=4))
+        wu_raw = keep_tile("wu_raw", F, I32)
+        nc.sync.dma_start(out=wu_raw[:], in_=wu_words[0].rearrange("p n t -> p (n t)").bitcast(I32))
+        vd_raw = []
+        for g in range(FG):
+            t = keep_tile(f"vd_raw{g}", 4 * D, BF16)
+            nc.sync.dma_start(out=t[:], in_=vd.rearrange("(g p j) n -> g p (j n)", p=P, j=4)[g])
+            vd_raw.append(t)
+        wd_q = keep_tile("wd_q", FG * D, I32)
+        nc.sync.dma_start(
+            out=wd_q[:].rearrange("p (g n) -> p g n", g=FG),
+            in_=wd_words.rearrange("g p n t -> p g (n t)").bitcast(I32),
+        )
+        for quad in range(4):
+            nc.sync.dma_start(
+                out=wd_sc[32 * quad : 32 * quad + 4, :].rearrange("r (g n) -> r g n", g=FG).bitcast(I32),
+                in_=wd_scales.rearrange("g r n -> r g n")[4 * quad : 4 * quad + 4].bitcast(I32),
+            )
+
+        def quantize(codes, scales, values):
+            nc.vector.quantize_mx(out=codes.bitcast(FP8X4), scales=scales, in_=values)
+
+        def bank(tag):
+            return psum.tile([P, CH], F32, name="bank_" + tag, tag=tag)
+
+        def by_channel(b):
+            return b[:].rearrange("p (t n) -> p n t", t=4)
+
+        def wide(ap):
+            return ap.rearrange("p (n t) -> p n t", t=4)
+
+        xq = keep_tile("xq", TOK, U32)
+        xs = keep_tile("xs", TOK, U8)
+        x_grp = []
+        for h in range(2):
+            t = bank("o")
+            words = x_raw[h][:].bitcast(F32)
+            for b in range(2):
+                for u in range(2):
+                    nc.tensor.transpose(
+                        t[:, (2 * b + u) * P : (2 * b + u + 1) * P],
+                        words[:, 256 * b + u : 256 * (b + 1) : 2],
+                        ident[:],
+                    )
+            grp = keep_tile(f"x_grp{h}", 8 * P, BF16)
+            nc.vector.tensor_copy(
+                out=grp[:].bitcast(F32).rearrange("p (b r u) -> p b r u", b=2, u=2),
+                in_=t[:].rearrange("p (b u r) -> p b r u", b=2, u=2),
+            )
+            x_grp.append(grp)
+        for h in range(2):
+            cols = slice(256 * h, 256 * (h + 1))
+            quantize(xq[:, cols], xs[:, cols], x_grp[h][:])
+
+        wg_q = keep_tile("wg_q", F, I32)
+        wu_q = keep_tile("wu_q", F, I32)
+        gu_sc = keep_tile("gu_sc", F, U8)
+
+        def permute(dst, src):
+            nc.vector.tensor_copy(
+                out=dst[:].rearrange("p (g t m) -> p g t m", g=FG, t=4),
+                in_=src[:].rearrange("p (g m t) -> p g t m", g=FG, t=4),
+            )
+
+        permute(wg_q, wg_raw)
+        permute(gu_sc, gu_scales_raw)
+
+        vg_w = keep_tile("vg_w", 4 * F, BF16)
+        for s in range(8):
+            for j in range(4):
+                cols = slice(j * F + s * P, j * F + (s + 1) * P)
+                codes = vg_b[:, cols].bitcast(F8)
+                scale = vg_s[:, 8 * j + s : 8 * j + s + 1]
+                if j < VW:
+                    nc.vector.tensor_scalar(out=vg_w[:, cols], in0=codes, scalar1=scale, scalar2=None, op0=ALU.mult)
+                else:
+                    nc.scalar.activation(out=vg_w[:, cols], in_=codes, func=ACT.Copy, scale=scale)
+
+        def up_views(grp, raw, g):
+            dst = grp[:, 4 * CH * g : 4 * CH * (g + 1)].rearrange("p (t m j) -> p t m j", t=4, j=4)
+            src = raw[:].rearrange("p (j g m t) -> p g t m j", j=4, g=FG, t=4)[:, g]
+            return dst, src
+
+        vu_grp = keep_tile("vu_grp", 4 * F, BF16)
+        vu_q = keep_tile("vu_q", F, U32)
+        vu_s = keep_tile("vu_s", F, U8)
+        vg_grp = keep_tile("vg_grp", 4 * F, BF16)
+        vg_q = keep_tile("vg_q", F, U32)
+        vg_sc = keep_tile("vg_sc", F, U8)
+        vd_grp = keep_tile("vd_grp", FG * 4 * D, BF16)
+        vd_q = keep_tile("vd_q", FG * D, U32)
+        vd_s = keep_tile("vd_s", FG * D, U8)
+
+        def stage1(tag, codes, scales, c):
+            tt, g = divmod(c, FG)
+            b = bank(tag)
+            toks = slice(P * tt, P * (tt + 1))
+            for t in range(4):
+                chans = slice(CH * g + P * t, CH * g + P * (t + 1))
+                nc.tensor.matmul_mx(
+                    out=b[:, P * t : P * (t + 1)],
+                    lhsT=codes[:, chans].bitcast(FP8X4),
+                    lhsT_scale=scales[:, chans],
+                    rhs=xq[:, toks].bitcast(FP8X4),
+                    rhs_scale=xs[:, toks],
+                    start=True,
+                    stop=True,
+                )
+            return b
+
+        act = [keep_tile(f"act{i}", 2 * CH, F32) for i in range(TT)]
+        sq = [keep_tile(f"sq{i}", 2 * CH, F32) for i in range(TT)]
+        lm = [keep_tile(f"lm{i}", 2 * CH, F32) for i in range(TT)]
+        au = [keep_tile(f"au{i}", 2 * CH, F32) for i in range(TT)]
+
+        def half(tiles, c):
+            tt, g = divmod(c, FG)
+            return tiles[tt][:, CH * g : CH * (g + 1)]
+
+        def square(c, b):
+            nc.scalar.activation(out=wide(half(sq, c)), in_=by_channel(b), func=ACT.Square, bias=TAU)
+
+        def gate(c):
+            b = stage1("g", wg_q, gu_sc[:, :], c)
+            nc.scalar.activation(out=wide(half(act, c)), in_=by_channel(b), func=ACT.Gelu, bias=TAU)
+            if c < 2 * NA:
+                square(c, b)
+
+        for c in range(4):
+            gate(c)
+
+        for g in range(FG):
+            dst, src = up_views(vu_grp, vu_raw, g)
+            nc.vector.tensor_copy(out=dst, in_=src)
+        permute(wu_q, wu_raw)
+        wu_sc = gu_sc[4:P, :]
+        quantize(vu_q[:], vu_s[:], vu_grp[:])
+
+        def turn(dst, src):
+            nc.gpsimd.tensor_scalar(out=dst, in0=src, scalar1=1.0, scalar2=0.0, op0=ALU.mult, op1=ALU.add)
+
+        for g in range(FG):
+            turn(*up_views(vg_grp, vg_w, g))
+        for g in range(FG):
+            turn(
+                vd_grp[:, 4 * D * g : 4 * D * (g + 1)].rearrange("p (n j) -> p n j", j=4),
+                vd_raw[g][:].rearrange("p (j n) -> p n j", j=4),
+            )
+
+        hb = [keep_tile(f"hb{i}", 2 * CH, BF16) for i in range(TT)]
+        hq = keep_tile("hq", TT * 256, U32)
+        hs = keep_tile("hs", TT * 256, U8)
+        db = [keep_tile(f"db{i}", 2 * CH, BF16) for i in range(TT)]
+        dq = keep_tile("dq", TT * 256, U32)
+        ds = keep_tile("ds", TT * 256, U8)
+
+        def quantize_tile(q, s, values, i):
+            cols = slice(256 * i, 256 * (i + 1))
+            quantize(q[:, cols], s[:, cols], values[i][:])
+
+        for c in range(8):
+            b = stage1("u", wu_q, wu_sc, c)
+            d = stage1("d", vu_q, vu_s, c)
+            if c + 4 < 8:
+                gate(c + 4)
+            nc.vector.tensor_tensor(out=wide(half(hb, c)), in0=wide(half(act, c)), in1=by_channel(b), op=ALU.mult)
+            nc.vector.tensor_tensor(out=wide(half(au, c)), in0=wide(half(act, c)), in1=by_channel(d), op=ALU.mult)
+            if c % 2 == 0 and c > 0:
+                quantize_tile(hq, hs, hb, c // 2 - 1)
+        quantize(vg_q[:], vg_sc[:], vg_grp[:])
+        quantize_tile(hq, hs, hb, TT - 1)
+
+        for tiles in (range(NA), range(NA, TT)):
+            for i in tiles:
+                if i >= NA:
+                    for c in (2 * i, 2 * i + 1):
+                        square(c, stage1("o", wg_q, gu_sc[:, :], c))
+            for i in tiles:
+                nc.scalar.activation(out=lm[i][:], in_=sq[i][:], func=ACT.Ln)
+            for i in tiles:
+                for c in range(FG):
+                    cols = slice(CH * c, CH * (c + 1))
+                    lo, so = lm[i][:, cols], sq[i][:, cols]
+                    nc.scalar.activation(out=lo, in_=lo, func=ACT.Exp, scale=-1.0)
+                    nc.scalar.activation(out=so, in_=so, func=ACT.Exp, scale=-0.5, bias=LOG_C)
+                    eng = nc.vector if (i == 0 and c == 0) else nc.gpsimd
+                    eng.tensor_tensor(out=lo, in0=lo, in1=act[i][:, cols], op=ALU.mult)
+                    eng.tensor_tensor(out=lo, in0=lo, in1=so, op=ALU.add)
+
+        def stage2(i):
+            b = bank("o")
+            toks = [slice(256 * i + P * g, 256 * i + P * (g + 1)) for g in range(FG)]
+            outs = [slice(D * g, D * (g + 1)) for g in range(FG)]
+            passes = [(hq, hs, vd_q, vd_s, g) for g in range(FG)] + [(dq, ds, wd_q, wd_sc, g) for g in range(FG)]
+            for n, (lq, ls, rq, rs, g) in enumerate(passes):
+                nc.tensor.matmul_mx(
+                    out=b[:],
+                    lhsT=lq[:, toks[g]].bitcast(FP8X4),
+                    lhsT_scale=ls[:, toks[g]],
+                    rhs=rq[:, outs[g]].bitcast(FP8X4),
+                    rhs_scale=rs[:, outs[g]],
+                    start=(n == 0),
+                    stop=(n == len(passes) - 1),
+                )
+            res = work.tile([P, D], F32, name="res")
+            nc.scalar.copy(out=res[:], in_=b[:])
+            nc.sync.dma_start(out=out[P * i : P * (i + 1), :], in_=res[:])
+
+        for i in range(TT):
+            pair = (2 * i, 2 * i + 1)
+            bg = [stage1("g", wg_q, gu_sc[:, :], c) for c in pair]
+            bd = [stage1("d", vg_q, vg_sc, c) for c in pair]
+            bu = [stage1("u", wu_q, wu_sc, c) for c in pair]
+            c1 = [work.tile([P, CH], F32, name=f"c{k}") for k in range(2)]
+            c2 = [work.tile([P, CH], F32, name=f"d{k}") for k in range(2)]
+            c3 = work.tile([P, 2 * CH], F32, name="e")
+            for k in range(2):
+                nc.vector.scalar_tensor_tensor(
+                    out=wide(c1[k][:]), in0=by_channel(bg[k]), scalar=TAU, in1=wide(half(lm, pair[k])), op0=ALU.add, op1=ALU.mult
+                )
+                if i == 0 and k == 0:
+                    quantize(vd_q[:], vd_s[:], vd_grp[:])
+            if i > 0:
+                quantize_tile(dq, ds, db, i - 1)
+                stage2(i - 1)
+            for k in range(2):
+                nc.vector.tensor_tensor(out=wide(c2[k][:]), in0=wide(c1[k][:]), in1=by_channel(bd[k]), op=ALU.mult)
+            for k in range(2):
+                nc.vector.tensor_tensor(
+                    out=wide(c3[:, CH * k : CH * (k + 1)]), in0=wide(c2[k][:]), in1=by_channel(bu[k]), op=ALU.mult
+                )
+            nc.vector.tensor_tensor(out=db[i][:], in0=c3[:], in1=au[i][:], op=ALU.add)
+        quantize_tile(dq, ds, db, TT - 1)
+        stage2(TT - 1)

@@ -3,306 +3,424 @@ from contextlib import ExitStack
 import concourse.mybir as mybir
 from concourse.masks import make_identity
 
-TOK, D, F = 512, 512, 1024
-FLOPS = 2 * TOK * D * F * 6
+TOKENS, D, F = 512, 512, 1024
+FLOPS = 6 * 2 * TOKENS * D * F
 
 F32 = mybir.dt.float32
 BF16 = mybir.dt.bfloat16
 I32 = mybir.dt.int32
 U32 = mybir.dt.uint32
 U8 = mybir.dt.uint8
-F8 = mybir.dt.float8_e4m3fn
+FP8 = mybir.dt.float8_e4m3fn
 FP8X4 = mybir.dt.float8_e4m3fn_x4
 ACT = mybir.ActivationFunctionType
 ALU = mybir.AluOpType
 
 P = 128
-TT = TOK // P
-FG = F // 512
-CH = 512
-VW = 1
-NA = 3
+PACK = 4
+GROUP = P * PACK
+TILES = TOKENS // P
+GROUPS = F // GROUP
+CHUNKS = TILES * GROUPS
+SCALE_RUN = 128
+RUNS = F // SCALE_RUN
+
 TAU = 2.5e-10
-LOG_C = -0.9189385332046727
+LOG_DENSITY = -0.9189385332046727
+
+GATES_AHEAD = 6
+VECTOR_SLOPES = 2
+SLOPES_AHEAD = 4
+FIRST_DOWN = 5
 
 
 def tile_forwardgradientgegluweighttangent_d1p_kernel(
     tc, x, wg_words, wg_scales, vg_bytes, vg_scale, wu_words, wu_scales, vu, wd_words, wd_scales, vd, out
 ):
     nc = tc.nc
+
     with ExitStack() as ctx:
         keep = ctx.enter_context(tc.tile_pool(name="keep", bufs=1))
         work = ctx.enter_context(tc.tile_pool(name="work", bufs=2))
         psum = ctx.enter_context(tc.psum_pool(name="psum", bufs=2))
         ctx.enter_context(tc.manual_schedule())
 
-        def keep_tile(name, cols, dtype):
-            return keep.tile([P, cols], dtype, name=name, align_bytes=64)
-
-        x_raw = []
-        for h in range(2):
-            t = keep_tile(f"x_raw{h}", 2 * D, BF16)
-            nc.sync.dma_start(
-                out=t[:].rearrange("p (b d) -> p b d", b=2),
-                in_=x.rearrange("(h b p) d -> h p b d", b=2, p=P)[h],
-            )
-            x_raw.append(t)
-        vg_s = keep_tile("vg_s", 32, F32)
-        nc.sync.dma_start(out=vg_s[:], in_=vg_scale.rearrange("(p j) s -> p (j s)", j=4))
-        vg_b = keep_tile("vg_b", 4 * F, U8)
-        nc.sync.dma_start(out=vg_b[:], in_=vg_bytes.rearrange("(p j) f -> p (j f)", j=4))
-        wg_raw = keep_tile("wg_raw", F, I32)
-        nc.sync.dma_start(out=wg_raw[:], in_=wg_words[0].rearrange("p n t -> p (n t)").bitcast(I32))
-
-        warm = keep_tile("warm", 1, F32)
-        nc.vector.memset(warm[:], 0.0)
-        nc.scalar.activation(out=warm[:], in_=warm[:], func=ACT.Gelu)
-        gu_scales_raw = keep_tile("gu_scales_raw", F, U8)
-        wd_sc = keep_tile("wd_sc", FG * D, U8)
-        nc.vector.memset(gu_scales_raw[:].bitcast(I32), 0)
-        nc.vector.memset(wd_sc[:].bitcast(I32), 0)
-        ident = keep_tile("ident", P, F32)
-        make_identity(nc, ident[:])
-        for first, scales in ((0, wg_scales), (4, wu_scales)):
-            for quad in range(4):
-                rows = slice(32 * quad + first, 32 * quad + first + 4)
-                nc.scalar.dma_start(
-                    out=gu_scales_raw[rows, :].bitcast(I32),
-                    in_=scales[0, 4 * quad : 4 * quad + 4, :].bitcast(I32),
-                )
-
-        vu_raw = keep_tile("vu_raw", 4 * F, BF16)
-        nc.sync.dma_start(out=vu_raw[:], in_=vu.rearrange("(p j) f -> p (j f)", j=4))
-        wu_raw = keep_tile("wu_raw", F, I32)
-        nc.sync.dma_start(out=wu_raw[:], in_=wu_words[0].rearrange("p n t -> p (n t)").bitcast(I32))
-        vd_raw = []
-        for g in range(FG):
-            t = keep_tile(f"vd_raw{g}", 4 * D, BF16)
-            nc.sync.dma_start(out=t[:], in_=vd.rearrange("(g p j) n -> g p (j n)", p=P, j=4)[g])
-            vd_raw.append(t)
-        wd_q = keep_tile("wd_q", FG * D, I32)
-        nc.sync.dma_start(
-            out=wd_q[:].rearrange("p (g n) -> p g n", g=FG),
-            in_=wd_words.rearrange("g p n t -> p g (n t)").bitcast(I32),
-        )
-        for quad in range(4):
-            nc.sync.dma_start(
-                out=wd_sc[32 * quad : 32 * quad + 4, :].rearrange("r (g n) -> r g n", g=FG).bitcast(I32),
-                in_=wd_scales.rearrange("g r n -> r g n")[4 * quad : 4 * quad + 4].bitcast(I32),
-            )
-
-        def quantize(codes, scales, values):
-            nc.vector.quantize_mx(out=codes.bitcast(FP8X4), scales=scales, in_=values)
+        def keep_tile(name, columns, dtype):
+            return keep.tile([P, columns], dtype, name=name, align_bytes=64)
 
         def bank(tag):
-            return psum.tile([P, CH], F32, name="bank_" + tag, tag=tag)
+            return psum.tile([P, GROUP], F32, name="bank_" + tag, tag=tag)
 
-        def by_channel(b):
-            return b[:].rearrange("p (t n) -> p n t", t=4)
+        x_raw = [keep_tile(f"x_raw{k}", 2 * D, BF16) for k in range(2)]
+        vg_raw = keep_tile("vg_raw", PACK * F, U8)
+        vg_run_scale = keep_tile("vg_run_scale", PACK * RUNS, F32)
+        vu_raw = keep_tile("vu_raw", PACK * F, BF16)
+        vd_raw = keep_tile("vd_raw", GROUPS * PACK * D, BF16)
+        wg_codes = keep_tile("wg_codes", F, I32)
+        wu_codes = keep_tile("wu_codes", F, I32)
+        wd_codes = keep_tile("wd_codes", GROUPS * D, I32)
+        wg_plane = keep_tile("wg_plane", F, U8)
+        wu_plane = keep_tile("wu_plane", F, U8)
+        wd_plane = keep_tile("wd_plane", GROUPS * D, U8)
 
-        def wide(ap):
-            return ap.rearrange("p (n t) -> p n t", t=4)
+        for plane in (wg_plane, wu_plane, wd_plane):
+            nc.vector.memset(plane[:].bitcast(I32), 0)
+        identity = keep_tile("identity", P, F32)
+        make_identity(nc, identity[:])
 
-        xq = keep_tile("xq", TOK, U32)
-        xs = keep_tile("xs", TOK, U8)
-        x_grp = []
-        for h in range(2):
-            t = bank("o")
-            words = x_raw[h][:].bitcast(F32)
+        def load_codes(codes, words):
+            nc.sync.dma_start(
+                out=codes[:].rearrange("p (g n) -> p g n", g=words.shape[0]),
+                in_=words.rearrange("g p n t -> p g (n t)").bitcast(I32),
+            )
+
+        def load_plane(engine, plane, scales):
+            for q in range(4):
+                engine.dma_start(
+                    out=plane[32 * q : 32 * q + 4, :].rearrange("r (g n) -> r g n", g=scales.shape[0]).bitcast(I32),
+                    in_=scales.rearrange("g r n -> r g n")[4 * q : 4 * q + 4].bitcast(I32),
+                )
+
+        nc.sync.dma_start(out=vg_run_scale[:], in_=vg_scale.rearrange("(p t) s -> p (t s)", t=PACK))
+        for k in range(2):
+            nc.sync.dma_start(
+                out=x_raw[k][:].rearrange("p (b d) -> p b d", b=2),
+                in_=x.rearrange("(k b p) d -> k p b d", b=2, p=P)[k],
+            )
+        nc.sync.dma_start(out=vg_raw[:], in_=vg_bytes.rearrange("(p t) f -> p (t f)", t=PACK))
+        load_codes(wg_codes, wg_words)
+        load_plane(nc.scalar, wg_plane, wg_scales)
+        nc.sync.dma_start(out=vu_raw[:], in_=vu.rearrange("(p t) f -> p (t f)", t=PACK))
+        load_codes(wu_codes, wu_words)
+        load_plane(nc.sync, wu_plane, wu_scales)
+        nc.sync.dma_start(
+            out=vd_raw[:].rearrange("p (g r) -> p g r", g=GROUPS),
+            in_=vd.rearrange("(g p t) n -> p g (t n)", p=P, t=PACK),
+        )
+        load_codes(wd_codes, wd_words)
+        load_plane(nc.sync, wd_plane, wd_scales)
+
+        def operand(name, columns):
+            return keep_tile(name + "_codes", columns, U32), keep_tile(name + "_plane", columns, U8)
+
+        x_codes, x_plane = operand("x", TOKENS)
+        vu_codes, vu_plane = operand("vu", F)
+        vg_codes, vg_plane = operand("vg", F)
+        vd_codes, vd_plane = operand("vd", GROUPS * D)
+        h_codes, h_plane = operand("h", CHUNKS * P)
+        dh_codes, dh_plane = operand("dh", CHUNKS * P)
+
+        def quantize(codes, plane, values, lo, hi):
+            nc.vector.quantize_mx(
+                out=codes[:, lo:hi].bitcast(FP8X4), scales=plane[:, lo:hi], in_=values[:, PACK * lo : PACK * hi]
+            )
+
+        x_grouped = keep_tile("x_grouped", PACK * TOKENS, BF16)
+        pair = 2 * P
+        for k, copy in enumerate((nc.vector.tensor_copy, nc.scalar.copy)):
+            turned = bank("turn")
+            words = x_raw[k][:].bitcast(F32)
             for b in range(2):
                 for u in range(2):
                     nc.tensor.transpose(
-                        t[:, (2 * b + u) * P : (2 * b + u + 1) * P],
-                        words[:, 256 * b + u : 256 * (b + 1) : 2],
-                        ident[:],
+                        turned[:, P * (2 * b + u) : P * (2 * b + u + 1)],
+                        words[:, D // 2 * b + u : D // 2 * (b + 1) : 2],
+                        identity[:],
                     )
-            grp = keep_tile(f"x_grp{h}", 8 * P, BF16)
-            nc.vector.tensor_copy(
-                out=grp[:].bitcast(F32).rearrange("p (b r u) -> p b r u", b=2, u=2),
-                in_=t[:].rearrange("p (b u r) -> p b r u", b=2, u=2),
+            copy(
+                out=x_grouped[:, PACK * pair * k : PACK * pair * (k + 1)]
+                .bitcast(F32)
+                .rearrange("p (b n u) -> p b n u", b=2, u=2),
+                in_=turned[:].rearrange("p (b u n) -> p b n u", b=2, u=2),
             )
-            x_grp.append(grp)
-        for h in range(2):
-            cols = slice(256 * h, 256 * (h + 1))
-            quantize(xq[:, cols], xs[:, cols], x_grp[h][:])
+        for k in range(2):
+            quantize(x_codes, x_plane, x_grouped, pair * k, pair * (k + 1))
 
-        wg_q = keep_tile("wg_q", F, I32)
-        wu_q = keep_tile("wu_q", F, I32)
-        gu_sc = keep_tile("gu_sc", F, U8)
-
-        def permute(dst, src):
-            nc.vector.tensor_copy(
-                out=dst[:].rearrange("p (g t m) -> p g t m", g=FG, t=4),
-                in_=src[:].rearrange("p (g m t) -> p g t m", g=FG, t=4),
-            )
-
-        permute(wg_q, wg_raw)
-        permute(gu_sc, gu_scales_raw)
-
-        vg_w = keep_tile("vg_w", 4 * F, BF16)
-        for s in range(8):
-            for j in range(4):
-                cols = slice(j * F + s * P, j * F + (s + 1) * P)
-                codes = vg_b[:, cols].bitcast(F8)
-                scale = vg_s[:, 8 * j + s : 8 * j + s + 1]
-                if j < VW:
-                    nc.vector.tensor_scalar(out=vg_w[:, cols], in0=codes, scalar1=scale, scalar2=None, op0=ALU.mult)
-                else:
-                    nc.scalar.activation(out=vg_w[:, cols], in_=codes, func=ACT.Copy, scale=scale)
-
-        def up_views(grp, raw, g):
-            dst = grp[:, 4 * CH * g : 4 * CH * (g + 1)].rearrange("p (t m j) -> p t m j", t=4, j=4)
-            src = raw[:].rearrange("p (j g m t) -> p g t m j", j=4, g=FG, t=4)[:, g]
-            return dst, src
-
-        vu_grp = keep_tile("vu_grp", 4 * F, BF16)
-        vu_q = keep_tile("vu_q", F, U32)
-        vu_s = keep_tile("vu_s", F, U8)
-        vg_grp = keep_tile("vg_grp", 4 * F, BF16)
-        vg_q = keep_tile("vg_q", F, U32)
-        vg_sc = keep_tile("vg_sc", F, U8)
-        vd_grp = keep_tile("vd_grp", FG * 4 * D, BF16)
-        vd_q = keep_tile("vd_q", FG * D, U32)
-        vd_s = keep_tile("vd_s", FG * D, U8)
-
-        def stage1(tag, codes, scales, c):
-            tt, g = divmod(c, FG)
-            b = bank(tag)
-            toks = slice(P * tt, P * (tt + 1))
-            for t in range(4):
-                chans = slice(CH * g + P * t, CH * g + P * (t + 1))
-                nc.tensor.matmul_mx(
-                    out=b[:, P * t : P * (t + 1)],
-                    lhsT=codes[:, chans].bitcast(FP8X4),
-                    lhsT_scale=scales[:, chans],
-                    rhs=xq[:, toks].bitcast(FP8X4),
-                    rhs_scale=xs[:, toks],
-                    start=True,
-                    stop=True,
+        vg_wide = keep_tile("vg_wide", PACK * F, BF16)
+        for run in range(RUNS):
+            for t in range(PACK):
+                columns = slice(F * t + SCALE_RUN * run, F * t + SCALE_RUN * (run + 1))
+                nc.vector.tensor_scalar(
+                    out=vg_wide[:, columns],
+                    in0=vg_raw[:, columns].bitcast(FP8),
+                    scalar1=vg_run_scale[:, RUNS * t + run : RUNS * t + run + 1],
+                    scalar2=None,
+                    op0=ALU.mult,
                 )
+
+        def vector_interleave(out_cols, in_cols):
+            nc.vector.tensor_copy(
+                out=out_cols.rearrange("p (c i t) -> p c t i", i=4, t=PACK),
+                in_=in_cols.rearrange("p (t c i) -> p c t i", i=4, t=PACK),
+            )
+
+        def gpsimd_interleave(out_cols, in_view):
+            nc.gpsimd.tensor_scalar(
+                out=out_cols.rearrange("p (n t) -> p n t", t=PACK),
+                in0=in_view,
+                scalar1=1.0,
+                scalar2=0.0,
+                op0=ALU.mult,
+                op1=ALU.add,
+            )
+
+        vu_grouped = keep_tile("vu_grouped", PACK * F, BF16)
+        vector_interleave(vu_grouped[:], vu_raw[:])
+        quantize(vu_codes, vu_plane, vu_grouped, 0, F)
+
+        def stage1(tag, codes, plane, chunk):
+            i, g = divmod(chunk, GROUPS)
+            tokens = slice(P * i, P * (i + 1))
+            channels = slice(GROUP * g, GROUP * (g + 1))
+            b = bank(tag)
+            nc.tensor.matmul_mx(
+                out=b[:],
+                lhsT=x_codes[:, tokens].bitcast(FP8X4),
+                lhsT_scale=x_plane[:, tokens],
+                rhs=codes[:, channels].bitcast(FP8X4),
+                rhs_scale=plane[:, channels],
+                start=True,
+                stop=True,
+            )
             return b
 
-        act = [keep_tile(f"act{i}", 2 * CH, F32) for i in range(TT)]
-        sq = [keep_tile(f"sq{i}", 2 * CH, F32) for i in range(TT)]
-        lm = [keep_tile(f"lm{i}", 2 * CH, F32) for i in range(TT)]
-        au = [keep_tile(f"au{i}", 2 * CH, F32) for i in range(TT)]
+        def bank_g(chunk):
+            return stage1("gate", wg_codes, wg_plane, chunk)
 
-        def half(tiles, c):
-            tt, g = divmod(c, FG)
-            return tiles[tt][:, CH * g : CH * (g + 1)]
+        def bank_u(chunk):
+            return stage1("up", wu_codes, wu_plane, chunk)
 
-        def square(c, b):
-            nc.scalar.activation(out=wide(half(sq, c)), in_=by_channel(b), func=ACT.Square, bias=TAU)
+        def bank_du(chunk):
+            return stage1("direction", vu_codes, vu_plane, chunk)
 
-        def gate(c):
-            b = stage1("g", wg_q, gu_sc[:, :], c)
-            nc.scalar.activation(out=wide(half(act, c)), in_=by_channel(b), func=ACT.Gelu, bias=TAU)
-            if c < 2 * NA:
-                square(c, b)
+        def bank_dg(chunk):
+            return stage1("direction", vg_codes, vg_plane, chunk)
 
-        for c in range(4):
-            gate(c)
+        def from_bank(b):
+            return b[:].rearrange("n (p t) -> n t p", t=PACK)
 
-        for g in range(FG):
-            dst, src = up_views(vu_grp, vu_raw, g)
-            nc.vector.tensor_copy(out=dst, in_=src)
-        permute(wu_q, wu_raw)
-        wu_sc = gu_sc[4:P, :]
-        quantize(vu_q[:], vu_s[:], vu_grp[:])
+        def in_order(columns):
+            return columns.rearrange("n (t p) -> n t p", t=PACK)
 
-        def turn(dst, src):
-            nc.gpsimd.tensor_scalar(out=dst, in0=src, scalar1=1.0, scalar2=0.0, op0=ALU.mult, op1=ALU.add)
+        def part(tiles, chunk):
+            i, g = divmod(chunk, GROUPS)
+            return tiles[i][:, GROUP * g : GROUP * (g + 1)]
 
-        for g in range(FG):
-            turn(*up_views(vg_grp, vg_w, g))
-        for g in range(FG):
-            turn(
-                vd_grp[:, 4 * D * g : 4 * D * (g + 1)].rearrange("p (n j) -> p n j", j=4),
-                vd_raw[g][:].rearrange("p (j n) -> p n j", j=4),
+        act = [keep_tile(f"act{i}", F, F32) for i in range(TILES)]
+        square = [keep_tile(f"square{i}", F, F32) for i in range(TILES)]
+        slope = [keep_tile(f"slope{i}", F, F32) for i in range(TILES)]
+        act_du = [keep_tile(f"act_du{i}", F, F32) for i in range(TILES)]
+        h = [keep_tile(f"h{i}", F, BF16) for i in range(TILES)]
+
+        def gate(chunk):
+            b = bank_g(chunk)
+            nc.scalar.activation(out=in_order(part(act, chunk)), in_=from_bank(b), func=ACT.Gelu, bias=TAU)
+            nc.scalar.activation(out=in_order(part(square, chunk)), in_=from_bank(b), func=ACT.Square, bias=TAU)
+
+        def hidden(chunk, b):
+            nc.vector.tensor_tensor(
+                out=part(h, chunk).rearrange("n (u p e) -> n u p e", u=2, e=2),
+                in0=part(act, chunk).rearrange("n (u e p) -> n u p e", u=2, e=2),
+                in1=b[:].rearrange("n (p u e) -> n u p e", u=2, e=2),
+                op=ALU.mult,
             )
 
-        hb = [keep_tile(f"hb{i}", 2 * CH, BF16) for i in range(TT)]
-        hq = keep_tile("hq", TT * 256, U32)
-        hs = keep_tile("hs", TT * 256, U8)
-        db = [keep_tile(f"db{i}", 2 * CH, BF16) for i in range(TT)]
-        dq = keep_tile("dq", TT * 256, U32)
-        ds = keep_tile("ds", TT * 256, U8)
+        for chunk in range(GATES_AHEAD):
+            gate(chunk)
 
-        def quantize_tile(q, s, values, i):
-            cols = slice(256 * i, 256 * (i + 1))
-            quantize(q[:, cols], s[:, cols], values[i][:])
+        vg_grouped = keep_tile("vg_grouped", PACK * F, BF16)
+        vd_grouped = keep_tile("vd_grouped", GROUPS * PACK * D, BF16)
+        vd_cols = [slice(PACK * D * g, PACK * D * (g + 1)) for g in range(GROUPS)]
+        gpsimd_interleave(vd_grouped[:, vd_cols[0]], vd_raw[:, vd_cols[0]].rearrange("p (t n) -> p n t", t=PACK))
+        for g in range(GROUPS):
+            gpsimd_interleave(
+                vg_grouped[:, PACK * GROUP * g : PACK * GROUP * (g + 1)],
+                vg_wide[:].rearrange("p (t g n) -> p g n t", t=PACK, g=GROUPS)[:, g],
+            )
 
-        for c in range(8):
-            b = stage1("u", wu_q, wu_sc, c)
-            d = stage1("d", vu_q, vu_s, c)
-            if c + 4 < 8:
-                gate(c + 4)
-            nc.vector.tensor_tensor(out=wide(half(hb, c)), in0=wide(half(act, c)), in1=by_channel(b), op=ALU.mult)
-            nc.vector.tensor_tensor(out=wide(half(au, c)), in0=wide(half(act, c)), in1=by_channel(d), op=ALU.mult)
-            if c % 2 == 0 and c > 0:
-                quantize_tile(hq, hs, hb, c // 2 - 1)
-        quantize(vg_q[:], vg_sc[:], vg_grp[:])
-        quantize_tile(hq, hs, hb, TT - 1)
+        for chunk in range(CHUNKS):
+            b_u = bank_u(chunk)
+            b_du = bank_du(chunk)
+            if chunk + GATES_AHEAD < CHUNKS:
+                gate(chunk + GATES_AHEAD)
+            hidden(chunk, b_u)
+            nc.vector.tensor_tensor(
+                out=in_order(part(act_du, chunk)), in0=in_order(part(act, chunk)), in1=from_bank(b_du), op=ALU.mult
+            )
 
-        for tiles in (range(NA), range(NA, TT)):
-            for i in tiles:
-                if i >= NA:
-                    for c in (2 * i, 2 * i + 1):
-                        square(c, stage1("o", wg_q, gu_sc[:, :], c))
-            for i in tiles:
-                nc.scalar.activation(out=lm[i][:], in_=sq[i][:], func=ACT.Ln)
-            for i in tiles:
-                for c in range(FG):
-                    cols = slice(CH * c, CH * (c + 1))
-                    lo, so = lm[i][:, cols], sq[i][:, cols]
-                    nc.scalar.activation(out=lo, in_=lo, func=ACT.Exp, scale=-1.0)
-                    nc.scalar.activation(out=so, in_=so, func=ACT.Exp, scale=-0.5, bias=LOG_C)
-                    eng = nc.vector if (i == 0 and c == 0) else nc.gpsimd
-                    eng.tensor_tensor(out=lo, in0=lo, in1=act[i][:, cols], op=ALU.mult)
-                    eng.tensor_tensor(out=lo, in0=lo, in1=so, op=ALU.add)
+        vector_interleave(vd_grouped[:, vd_cols[1]], vd_raw[:, vd_cols[1]])
+        quantize(vg_codes, vg_plane, vg_grouped, 0, F)
+        quantize(vd_codes, vd_plane, vd_grouped, 0, GROUPS * D)
 
-        def stage2(i):
-            b = bank("o")
-            toks = [slice(256 * i + P * g, 256 * i + P * (g + 1)) for g in range(FG)]
-            outs = [slice(D * g, D * (g + 1)) for g in range(FG)]
-            passes = [(hq, hs, vd_q, vd_s, g) for g in range(FG)] + [(dq, ds, wd_q, wd_sc, g) for g in range(FG)]
-            for n, (lq, ls, rq, rs, g) in enumerate(passes):
-                nc.tensor.matmul_mx(
-                    out=b[:],
-                    lhsT=lq[:, toks[g]].bitcast(FP8X4),
-                    lhsT_scale=ls[:, toks[g]],
-                    rhs=rq[:, outs[g]].bitcast(FP8X4),
-                    rhs_scale=rs[:, outs[g]],
-                    start=(n == 0),
-                    stop=(n == len(passes) - 1),
+        for i in range(TILES):
+            nc.scalar.activation(out=slope[i][:], in_=square[i][:], func=ACT.Ln)
+
+        def slope_exp(chunk):
+            m, s = part(slope, chunk), part(square, chunk)
+            nc.scalar.activation(out=m, in_=m, func=ACT.Exp, scale=-1.0)
+            nc.scalar.activation(out=s, in_=s, func=ACT.Exp, scale=-0.5, bias=LOG_DENSITY)
+
+        def slope_mul(engine, chunk):
+            m = part(slope, chunk)
+            engine.tensor_tensor(out=m, in0=m, in1=part(act, chunk), op=ALU.mult)
+
+        def slope_add(engine, chunk):
+            m = part(slope, chunk)
+            engine.tensor_tensor(out=m, in0=m, in1=part(square, chunk), op=ALU.add)
+
+        h_grouped = keep_tile("h_grouped", PACK * CHUNKS * P, BF16)
+        dh_grouped = keep_tile("dh_grouped", PACK * CHUNKS * P, BF16)
+
+        def turn_hidden(i):
+            b = bank("turn")
+            words = h[i][:].bitcast(F32)
+            for k in range(4):
+                nc.tensor.transpose(b[:, P * k : P * (k + 1)], words[:, P * k : P * (k + 1)], identity[:])
+            nc.scalar.copy(
+                out=h_grouped[:, F * i : F * (i + 1)]
+                .bitcast(F32)
+                .rearrange("p (g n u) -> p g n u", g=GROUPS, u=2),
+                in_=b[:].rearrange("p (g u n) -> p g n u", g=GROUPS, u=2),
+            )
+
+        c_out, d_out, e_out = {}, {}, {}
+        banks = {}
+
+        def fill(chunk):
+            banks[chunk] = (bank_g(chunk), bank_dg(chunk), bank_u(chunk))
+
+        def multiply_gate(chunk):
+            c_out[chunk] = work.tile([P, GROUP], F32, name="c_out")
+            nc.vector.scalar_tensor_tensor(
+                out=in_order(c_out[chunk][:]),
+                in0=from_bank(banks[chunk][0]),
+                scalar=TAU,
+                in1=in_order(part(slope, chunk)),
+                op0=ALU.add,
+                op1=ALU.mult,
+            )
+
+        def multiply_direction(chunk):
+            d_out[chunk] = work.tile([P, GROUP], F32, name="d_out")
+            nc.vector.tensor_tensor(
+                out=in_order(d_out[chunk][:]),
+                in0=in_order(c_out[chunk][:]),
+                in1=from_bank(banks[chunk][1]),
+                op=ALU.mult,
+            )
+
+        def multiply_up(chunk):
+            e_out[chunk] = work.tile([P, GROUP], F32, name="e_out")
+            nc.vector.tensor_tensor(
+                out=in_order(e_out[chunk][:]),
+                in0=in_order(d_out[chunk][:]),
+                in1=from_bank(banks[chunk][2]),
+                op=ALU.mult,
+            )
+
+        def turn_sum(chunk):
+            b = bank("turn")
+            for t in range(PACK):
+                columns = slice(P * t, P * (t + 1))
+                nc.tensor.matmul(
+                    b[:, columns],
+                    lhsT=part(act_du, chunk)[:, columns],
+                    rhs=identity[:],
+                    is_transpose=True,
+                    start=True,
+                    stop=False,
                 )
-            res = work.tile([P, D], F32, name="res")
-            nc.scalar.copy(out=res[:], in_=b[:])
-            nc.sync.dma_start(out=out[P * i : P * (i + 1), :], in_=res[:])
+                nc.tensor.matmul(
+                    b[:, columns],
+                    lhsT=e_out[chunk][:, columns],
+                    rhs=identity[:],
+                    is_transpose=True,
+                    start=False,
+                    stop=True,
+                )
+            nc.scalar.copy(
+                out=dh_grouped[:, GROUP * chunk : GROUP * (chunk + 1)].rearrange("p (n t) -> p n t", t=PACK),
+                in_=b[:].rearrange("p (t n) -> p n t", t=PACK),
+            )
 
-        for i in range(TT):
-            pair = (2 * i, 2 * i + 1)
-            bg = [stage1("g", wg_q, gu_sc[:, :], c) for c in pair]
-            bd = [stage1("d", vg_q, vg_sc, c) for c in pair]
-            bu = [stage1("u", wu_q, wu_sc, c) for c in pair]
-            c1 = [work.tile([P, CH], F32, name=f"c{k}") for k in range(2)]
-            c2 = [work.tile([P, CH], F32, name=f"d{k}") for k in range(2)]
-            c3 = work.tile([P, 2 * CH], F32, name="e")
-            for k in range(2):
-                nc.vector.scalar_tensor_tensor(
-                    out=wide(c1[k][:]), in0=by_channel(bg[k]), scalar=TAU, in1=wide(half(lm, pair[k])), op0=ALU.add, op1=ALU.mult
-                )
-                if i == 0 and k == 0:
-                    quantize(vd_q[:], vd_s[:], vd_grp[:])
-            if i > 0:
-                quantize_tile(dq, ds, db, i - 1)
-                stage2(i - 1)
-            for k in range(2):
-                nc.vector.tensor_tensor(out=wide(c2[k][:]), in0=wide(c1[k][:]), in1=by_channel(bd[k]), op=ALU.mult)
-            for k in range(2):
-                nc.vector.tensor_tensor(
-                    out=wide(c3[:, CH * k : CH * (k + 1)]), in0=wide(c2[k][:]), in1=by_channel(bu[k]), op=ALU.mult
-                )
-            nc.vector.tensor_tensor(out=db[i][:], in0=c3[:], in1=au[i][:], op=ALU.add)
-        quantize_tile(dq, ds, db, TT - 1)
-        stage2(TT - 1)
+        def quantize_dh(first, end):
+            quantize(dh_codes, dh_plane, dh_grouped, P * first, P * end)
+
+        terms = ((h_codes, h_plane, vd_codes, vd_plane), (dh_codes, dh_plane, wd_codes, wd_plane))
+
+        def down_pass(b, i, term, g, lo, hi):
+            left, left_plane, right, right_plane = terms[term]
+            tokens = slice(P * (GROUPS * i + g), P * (GROUPS * i + g + 1))
+            columns = slice(D * g + lo, D * g + hi)
+            nc.tensor.matmul_mx(
+                out=b[:, : hi - lo],
+                lhsT=left[:, tokens].bitcast(FP8X4),
+                lhsT_scale=left_plane[:, tokens],
+                rhs=right[:, columns].bitcast(FP8X4),
+                rhs_scale=right_plane[:, columns],
+                start=(term == 0 and g == 0),
+                stop=(term == 1 and g == GROUPS - 1),
+            )
+
+        def store(b, i, lo, hi, copy):
+            result = work.tile([P, hi - lo], F32, name=f"result{hi - lo}")
+            copy(out=result[:], in_=b[:, : hi - lo])
+            nc.sync.dma_start(out=out[P * i : P * (i + 1), lo:hi], in_=result[:])
+
+        def down(i):
+            b = bank("turn")
+            for term in range(2):
+                for g in range(GROUPS):
+                    down_pass(b, i, term, g, 0, D)
+            store(b, i, 0, D, nc.scalar.copy)
+
+        for chunk in range(SLOPES_AHEAD):
+            slope_exp(chunk)
+        for chunk in range(VECTOR_SLOPES):
+            slope_mul(nc.vector, chunk)
+        for chunk in range(VECTOR_SLOPES):
+            slope_add(nc.vector, chunk)
+
+        fill(0)
+        multiply_gate(0)
+        fill(1)
+        last = TILES - 1
+        for chunk in range(CHUNKS):
+            if chunk + VECTOR_SLOPES < CHUNKS:
+                slope_mul(nc.gpsimd, chunk + VECTOR_SLOPES)
+            if chunk > 0:
+                multiply_up(chunk - 1)
+            if chunk + VECTOR_SLOPES < CHUNKS:
+                slope_add(nc.gpsimd, chunk + VECTOR_SLOPES)
+            multiply_direction(chunk)
+            if 1 <= chunk <= TILES:
+                turn_hidden(chunk - 1)
+                slope_exp(chunk - 1 + SLOPES_AHEAD)
+            if chunk == FIRST_DOWN:
+                quantize(h_codes, h_plane, h_grouped, 0, CHUNKS * P)
+            if chunk > 0:
+                if chunk + 1 < CHUNKS:
+                    fill(chunk + 1)
+                turn_sum(chunk - 1)
+            if chunk + 1 < CHUNKS:
+                multiply_gate(chunk + 1)
+            if chunk >= FIRST_DOWN:
+                i = chunk - FIRST_DOWN
+                quantize_dh(GROUPS * i, GROUPS * (i + 1))
+                if chunk + 1 < CHUNKS:
+                    down(i)
+
+        multiply_up(CHUNKS - 1)
+        turn_sum(CHUNKS - 1)
+        down(last - 1)
+        halves = ((bank("gate"), 0, D // 2, nc.scalar.copy), (bank("direction"), D // 2, D, nc.vector.tensor_copy))
+        for b, lo, hi, copy in halves:
+            for g in range(GROUPS):
+                down_pass(b, last, 0, g, lo, hi)
+        for chunk in range(GROUPS * last, CHUNKS):
+            quantize_dh(chunk, chunk + 1)
+        for g in range(GROUPS):
+            for b, lo, hi, copy in halves:
+                down_pass(b, last, 1, g, lo, hi)
+        for b, lo, hi, copy in halves:
+            store(b, last, lo, hi, copy)

from contextlib import ExitStack

import concourse.mybir as mybir
from concourse.masks import make_identity

TOKENS, D, F = 512, 512, 1024
FLOPS = 6 * 2 * TOKENS * D * F

F32 = mybir.dt.float32
BF16 = mybir.dt.bfloat16
I32 = mybir.dt.int32
U32 = mybir.dt.uint32
U8 = mybir.dt.uint8
FP8 = mybir.dt.float8_e4m3fn
FP8X4 = mybir.dt.float8_e4m3fn_x4
ACT = mybir.ActivationFunctionType
ALU = mybir.AluOpType

P = 128
PACK = 4
GROUP = P * PACK
TILES = TOKENS // P
GROUPS = F // GROUP
CHUNKS = TILES * GROUPS
SCALE_RUN = 128
RUNS = F // SCALE_RUN

TAU = 2.5e-10
LOG_DENSITY = -0.9189385332046727

GATES_AHEAD = 6
VECTOR_SLOPES = 2
SLOPES_AHEAD = 4
FIRST_DOWN = 5


def tile_forwardgradientgegluweighttangent_d1p_kernel(
    tc, x, wg_words, wg_scales, vg_bytes, vg_scale, wu_words, wu_scales, vu, wd_words, wd_scales, vd, out
):
    nc = tc.nc

    with ExitStack() as ctx:
        keep = ctx.enter_context(tc.tile_pool(name="keep", bufs=1))
        work = ctx.enter_context(tc.tile_pool(name="work", bufs=2))
        psum = ctx.enter_context(tc.psum_pool(name="psum", bufs=2))
        ctx.enter_context(tc.manual_schedule())

        def keep_tile(name, columns, dtype):
            return keep.tile([P, columns], dtype, name=name, align_bytes=64)

        def bank(tag):
            return psum.tile([P, GROUP], F32, name="bank_" + tag, tag=tag)

        x_raw = [keep_tile(f"x_raw{k}", 2 * D, BF16) for k in range(2)]
        vg_raw = keep_tile("vg_raw", PACK * F, U8)
        vg_run_scale = keep_tile("vg_run_scale", PACK * RUNS, F32)
        vu_raw = keep_tile("vu_raw", PACK * F, BF16)
        vd_raw = keep_tile("vd_raw", GROUPS * PACK * D, BF16)
        wg_codes = keep_tile("wg_codes", F, I32)
        wu_codes = keep_tile("wu_codes", F, I32)
        wd_codes = keep_tile("wd_codes", GROUPS * D, I32)
        wg_plane = keep_tile("wg_plane", F, U8)
        wu_plane = keep_tile("wu_plane", F, U8)
        wd_plane = keep_tile("wd_plane", GROUPS * D, U8)

        for plane in (wg_plane, wu_plane, wd_plane):
            nc.vector.memset(plane[:].bitcast(I32), 0)
        identity = keep_tile("identity", P, F32)
        make_identity(nc, identity[:])

        def load_codes(codes, words):
            nc.sync.dma_start(
                out=codes[:].rearrange("p (g n) -> p g n", g=words.shape[0]),
                in_=words.rearrange("g p n t -> p g (n t)").bitcast(I32),
            )

        def load_plane(engine, plane, scales):
            for q in range(4):
                engine.dma_start(
                    out=plane[32 * q : 32 * q + 4, :].rearrange("r (g n) -> r g n", g=scales.shape[0]).bitcast(I32),
                    in_=scales.rearrange("g r n -> r g n")[4 * q : 4 * q + 4].bitcast(I32),
                )

        nc.sync.dma_start(out=vg_run_scale[:], in_=vg_scale.rearrange("(p t) s -> p (t s)", t=PACK))
        for k in range(2):
            nc.sync.dma_start(
                out=x_raw[k][:].rearrange("p (b d) -> p b d", b=2),
                in_=x.rearrange("(k b p) d -> k p b d", b=2, p=P)[k],
            )
        nc.sync.dma_start(out=vg_raw[:], in_=vg_bytes.rearrange("(p t) f -> p (t f)", t=PACK))
        load_codes(wg_codes, wg_words)
        load_plane(nc.scalar, wg_plane, wg_scales)
        nc.sync.dma_start(out=vu_raw[:], in_=vu.rearrange("(p t) f -> p (t f)", t=PACK))
        load_codes(wu_codes, wu_words)
        load_plane(nc.sync, wu_plane, wu_scales)
        nc.sync.dma_start(
            out=vd_raw[:].rearrange("p (g r) -> p g r", g=GROUPS),
            in_=vd.rearrange("(g p t) n -> p g (t n)", p=P, t=PACK),
        )
        load_codes(wd_codes, wd_words)
        load_plane(nc.sync, wd_plane, wd_scales)

        def operand(name, columns):
            return keep_tile(name + "_codes", columns, U32), keep_tile(name + "_plane", columns, U8)

        x_codes, x_plane = operand("x", TOKENS)
        vu_codes, vu_plane = operand("vu", F)
        vg_codes, vg_plane = operand("vg", F)
        vd_codes, vd_plane = operand("vd", GROUPS * D)
        h_codes, h_plane = operand("h", CHUNKS * P)
        dh_codes, dh_plane = operand("dh", CHUNKS * P)

        def quantize(codes, plane, values, lo, hi):
            nc.vector.quantize_mx(
                out=codes[:, lo:hi].bitcast(FP8X4), scales=plane[:, lo:hi], in_=values[:, PACK * lo : PACK * hi]
            )

        x_grouped = keep_tile("x_grouped", PACK * TOKENS, BF16)
        pair = 2 * P
        for k, copy in enumerate((nc.vector.tensor_copy, nc.scalar.copy)):
            turned = bank("turn")
            words = x_raw[k][:].bitcast(F32)
            for b in range(2):
                for u in range(2):
                    nc.tensor.transpose(
                        turned[:, P * (2 * b + u) : P * (2 * b + u + 1)],
                        words[:, D // 2 * b + u : D // 2 * (b + 1) : 2],
                        identity[:],
                    )
            copy(
                out=x_grouped[:, PACK * pair * k : PACK * pair * (k + 1)]
                .bitcast(F32)
                .rearrange("p (b n u) -> p b n u", b=2, u=2),
                in_=turned[:].rearrange("p (b u n) -> p b n u", b=2, u=2),
            )
        for k in range(2):
            quantize(x_codes, x_plane, x_grouped, pair * k, pair * (k + 1))

        vg_wide = keep_tile("vg_wide", PACK * F, BF16)
        for run in range(RUNS):
            for t in range(PACK):
                columns = slice(F * t + SCALE_RUN * run, F * t + SCALE_RUN * (run + 1))
                nc.vector.tensor_scalar(
                    out=vg_wide[:, columns],
                    in0=vg_raw[:, columns].bitcast(FP8),
                    scalar1=vg_run_scale[:, RUNS * t + run : RUNS * t + run + 1],
                    scalar2=None,
                    op0=ALU.mult,
                )

        def vector_interleave(out_cols, in_cols):
            nc.vector.tensor_copy(
                out=out_cols.rearrange("p (c i t) -> p c t i", i=4, t=PACK),
                in_=in_cols.rearrange("p (t c i) -> p c t i", i=4, t=PACK),
            )

        def gpsimd_interleave(out_cols, in_view):
            nc.gpsimd.tensor_scalar(
                out=out_cols.rearrange("p (n t) -> p n t", t=PACK),
                in0=in_view,
                scalar1=1.0,
                scalar2=0.0,
                op0=ALU.mult,
                op1=ALU.add,
            )

        vu_grouped = keep_tile("vu_grouped", PACK * F, BF16)
        vector_interleave(vu_grouped[:], vu_raw[:])
        quantize(vu_codes, vu_plane, vu_grouped, 0, F)

        def stage1(tag, codes, plane, chunk):
            i, g = divmod(chunk, GROUPS)
            tokens = slice(P * i, P * (i + 1))
            channels = slice(GROUP * g, GROUP * (g + 1))
            b = bank(tag)
            nc.tensor.matmul_mx(
                out=b[:],
                lhsT=x_codes[:, tokens].bitcast(FP8X4),
                lhsT_scale=x_plane[:, tokens],
                rhs=codes[:, channels].bitcast(FP8X4),
                rhs_scale=plane[:, channels],
                start=True,
                stop=True,
            )
            return b

        def bank_g(chunk):
            return stage1("gate", wg_codes, wg_plane, chunk)

        def bank_u(chunk):
            return stage1("up", wu_codes, wu_plane, chunk)

        def bank_du(chunk):
            return stage1("direction", vu_codes, vu_plane, chunk)

        def bank_dg(chunk):
            return stage1("direction", vg_codes, vg_plane, chunk)

        def from_bank(b):
            return b[:].rearrange("n (p t) -> n t p", t=PACK)

        def in_order(columns):
            return columns.rearrange("n (t p) -> n t p", t=PACK)

        def part(tiles, chunk):
            i, g = divmod(chunk, GROUPS)
            return tiles[i][:, GROUP * g : GROUP * (g + 1)]

        act = [keep_tile(f"act{i}", F, F32) for i in range(TILES)]
        square = [keep_tile(f"square{i}", F, F32) for i in range(TILES)]
        slope = [keep_tile(f"slope{i}", F, F32) for i in range(TILES)]
        act_du = [keep_tile(f"act_du{i}", F, F32) for i in range(TILES)]
        h = [keep_tile(f"h{i}", F, BF16) for i in range(TILES)]

        def gate(chunk):
            b = bank_g(chunk)
            nc.scalar.activation(out=in_order(part(act, chunk)), in_=from_bank(b), func=ACT.Gelu, bias=TAU)
            nc.scalar.activation(out=in_order(part(square, chunk)), in_=from_bank(b), func=ACT.Square, bias=TAU)

        def hidden(chunk, b):
            nc.vector.tensor_tensor(
                out=part(h, chunk).rearrange("n (u p e) -> n u p e", u=2, e=2),
                in0=part(act, chunk).rearrange("n (u e p) -> n u p e", u=2, e=2),
                in1=b[:].rearrange("n (p u e) -> n u p e", u=2, e=2),
                op=ALU.mult,
            )

        for chunk in range(GATES_AHEAD):
            gate(chunk)

        vg_grouped = keep_tile("vg_grouped", PACK * F, BF16)
        vd_grouped = keep_tile("vd_grouped", GROUPS * PACK * D, BF16)
        vd_cols = [slice(PACK * D * g, PACK * D * (g + 1)) for g in range(GROUPS)]
        gpsimd_interleave(vd_grouped[:, vd_cols[0]], vd_raw[:, vd_cols[0]].rearrange("p (t n) -> p n t", t=PACK))
        for g in range(GROUPS):
            gpsimd_interleave(
                vg_grouped[:, PACK * GROUP * g : PACK * GROUP * (g + 1)],
                vg_wide[:].rearrange("p (t g n) -> p g n t", t=PACK, g=GROUPS)[:, g],
            )

        for chunk in range(CHUNKS):
            b_u = bank_u(chunk)
            b_du = bank_du(chunk)
            if chunk + GATES_AHEAD < CHUNKS:
                gate(chunk + GATES_AHEAD)
            hidden(chunk, b_u)
            nc.vector.tensor_tensor(
                out=in_order(part(act_du, chunk)), in0=in_order(part(act, chunk)), in1=from_bank(b_du), op=ALU.mult
            )

        vector_interleave(vd_grouped[:, vd_cols[1]], vd_raw[:, vd_cols[1]])
        quantize(vg_codes, vg_plane, vg_grouped, 0, F)
        quantize(vd_codes, vd_plane, vd_grouped, 0, GROUPS * D)

        for i in range(TILES):
            nc.scalar.activation(out=slope[i][:], in_=square[i][:], func=ACT.Ln)

        def slope_exp(chunk):
            m, s = part(slope, chunk), part(square, chunk)
            nc.scalar.activation(out=m, in_=m, func=ACT.Exp, scale=-1.0)
            nc.scalar.activation(out=s, in_=s, func=ACT.Exp, scale=-0.5, bias=LOG_DENSITY)

        def slope_mul(engine, chunk):
            m = part(slope, chunk)
            engine.tensor_tensor(out=m, in0=m, in1=part(act, chunk), op=ALU.mult)

        def slope_add(engine, chunk):
            m = part(slope, chunk)
            engine.tensor_tensor(out=m, in0=m, in1=part(square, chunk), op=ALU.add)

        h_grouped = keep_tile("h_grouped", PACK * CHUNKS * P, BF16)
        dh_grouped = keep_tile("dh_grouped", PACK * CHUNKS * P, BF16)

        def turn_hidden(i):
            b = bank("turn")
            words = h[i][:].bitcast(F32)
            for k in range(4):
                nc.tensor.transpose(b[:, P * k : P * (k + 1)], words[:, P * k : P * (k + 1)], identity[:])
            nc.scalar.copy(
                out=h_grouped[:, F * i : F * (i + 1)]
                .bitcast(F32)
                .rearrange("p (g n u) -> p g n u", g=GROUPS, u=2),
                in_=b[:].rearrange("p (g u n) -> p g n u", g=GROUPS, u=2),
            )

        c_out, d_out, e_out = {}, {}, {}
        banks = {}

        def fill(chunk):
            banks[chunk] = (bank_g(chunk), bank_dg(chunk), bank_u(chunk))

        def multiply_gate(chunk):
            c_out[chunk] = work.tile([P, GROUP], F32, name="c_out")
            nc.vector.scalar_tensor_tensor(
                out=in_order(c_out[chunk][:]),
                in0=from_bank(banks[chunk][0]),
                scalar=TAU,
                in1=in_order(part(slope, chunk)),
                op0=ALU.add,
                op1=ALU.mult,
            )

        def multiply_direction(chunk):
            d_out[chunk] = work.tile([P, GROUP], F32, name="d_out")
            nc.vector.tensor_tensor(
                out=in_order(d_out[chunk][:]),
                in0=in_order(c_out[chunk][:]),
                in1=from_bank(banks[chunk][1]),
                op=ALU.mult,
            )

        def multiply_up(chunk):
            e_out[chunk] = work.tile([P, GROUP], F32, name="e_out")
            nc.vector.tensor_tensor(
                out=in_order(e_out[chunk][:]),
                in0=in_order(d_out[chunk][:]),
                in1=from_bank(banks[chunk][2]),
                op=ALU.mult,
            )

        def turn_sum(chunk):
            b = bank("turn")
            for t in range(PACK):
                columns = slice(P * t, P * (t + 1))
                nc.tensor.matmul(
                    b[:, columns],
                    lhsT=part(act_du, chunk)[:, columns],
                    rhs=identity[:],
                    is_transpose=True,
                    start=True,
                    stop=False,
                )
                nc.tensor.matmul(
                    b[:, columns],
                    lhsT=e_out[chunk][:, columns],
                    rhs=identity[:],
                    is_transpose=True,
                    start=False,
                    stop=True,
                )
            nc.scalar.copy(
                out=dh_grouped[:, GROUP * chunk : GROUP * (chunk + 1)].rearrange("p (n t) -> p n t", t=PACK),
                in_=b[:].rearrange("p (t n) -> p n t", t=PACK),
            )

        def quantize_dh(first, end):
            quantize(dh_codes, dh_plane, dh_grouped, P * first, P * end)

        terms = ((h_codes, h_plane, vd_codes, vd_plane), (dh_codes, dh_plane, wd_codes, wd_plane))

        def down_pass(b, i, term, g, lo, hi):
            left, left_plane, right, right_plane = terms[term]
            tokens = slice(P * (GROUPS * i + g), P * (GROUPS * i + g + 1))
            columns = slice(D * g + lo, D * g + hi)
            nc.tensor.matmul_mx(
                out=b[:, : hi - lo],
                lhsT=left[:, tokens].bitcast(FP8X4),
                lhsT_scale=left_plane[:, tokens],
                rhs=right[:, columns].bitcast(FP8X4),
                rhs_scale=right_plane[:, columns],
                start=(term == 0 and g == 0),
                stop=(term == 1 and g == GROUPS - 1),
            )

        def store(b, i, lo, hi, copy):
            result = work.tile([P, hi - lo], F32, name=f"result{hi - lo}")
            copy(out=result[:], in_=b[:, : hi - lo])
            nc.sync.dma_start(out=out[P * i : P * (i + 1), lo:hi], in_=result[:])

        def down(i):
            b = bank("turn")
            for term in range(2):
                for g in range(GROUPS):
                    down_pass(b, i, term, g, 0, D)
            store(b, i, 0, D, nc.scalar.copy)

        for chunk in range(SLOPES_AHEAD):
            slope_exp(chunk)
        for chunk in range(VECTOR_SLOPES):
            slope_mul(nc.vector, chunk)
        for chunk in range(VECTOR_SLOPES):
            slope_add(nc.vector, chunk)

        fill(0)
        multiply_gate(0)
        fill(1)
        last = TILES - 1
        for chunk in range(CHUNKS):
            if chunk + VECTOR_SLOPES < CHUNKS:
                slope_mul(nc.gpsimd, chunk + VECTOR_SLOPES)
            if chunk > 0:
                multiply_up(chunk - 1)
            if chunk + VECTOR_SLOPES < CHUNKS:
                slope_add(nc.gpsimd, chunk + VECTOR_SLOPES)
            multiply_direction(chunk)
            if 1 <= chunk <= TILES:
                turn_hidden(chunk - 1)
                slope_exp(chunk - 1 + SLOPES_AHEAD)
            if chunk == FIRST_DOWN:
                quantize(h_codes, h_plane, h_grouped, 0, CHUNKS * P)
            if chunk > 0:
                if chunk + 1 < CHUNKS:
                    fill(chunk + 1)
                turn_sum(chunk - 1)
            if chunk + 1 < CHUNKS:
                multiply_gate(chunk + 1)
            if chunk >= FIRST_DOWN:
                i = chunk - FIRST_DOWN
                quantize_dh(GROUPS * i, GROUPS * (i + 1))
                if chunk + 1 < CHUNKS:
                    down(i)

        multiply_up(CHUNKS - 1)
        turn_sum(CHUNKS - 1)
        down(last - 1)
        halves = ((bank("gate"), 0, D // 2, nc.scalar.copy), (bank("direction"), D // 2, D, nc.vector.tensor_copy))
        for b, lo, hi, copy in halves:
            for g in range(GROUPS):
                down_pass(b, last, 0, g, lo, hi)
        for chunk in range(GROUPS * last, CHUNKS):
            quantize_dh(chunk, chunk + 1)
        for g in range(GROUPS):
            for b, lo, hi, copy in halves:
                down_pass(b, last, 1, g, lo, hi)
        for b, lo, hi, copy in halves:
            store(b, last, lo, hi, copy)
